import numpy as np, ml_dtypes
CORES = [9,25,41,57]
N = 4
import mx_ref
BF = ml_dtypes.bfloat16
def gentries(a):
    return np.ascontiguousarray(a.reshape(8, 16, -1).transpose(0, 2, 1)).reshape(8, -1)
def gtable(e):
    e = np.asarray(e); return np.ascontiguousarray(e.reshape(8, -1, 16).transpose(0, 2, 1)).reshape(128, -1).astype(np.int32)
def gcols(t, e):
    v = np.concatenate([t.reshape(8, 16, -1, 4), np.zeros((8, 16, 1, 4), BF)], axis=2)
    return np.ascontiguousarray(np.stack([v[g][:, e[g]] for g in range(8)])).reshape(128, -1)
def tile(rs):
    return np.stack(rs, axis=2).reshape(128, -1).astype(BF)
def pick(q, e):
    c = np.concatenate([q[0].reshape(128, -1, 4), np.zeros((128, 1, 4), np.uint8)], axis=1); s = np.concatenate([q[1], np.ones((16, 1), np.uint8)], axis=1)
    return (np.ascontiguousarray(c[:, e].reshape(128, -1)), np.ascontiguousarray(s[:, e]))
def join(*qs):
    return (np.concatenate([q[0] for q in qs], axis=1), np.concatenate([q[1] for q in qs], axis=1))
def put(q, e, v):
    c, s = q[0].reshape(128, -1, 4).copy(), q[1].copy(); c[:, e] = v[0].reshape(128, -1, 4); s[:, e] = v[1]
    return (c.reshape(128, -1), s)
def pk(c, s):
    return (np.ascontiguousarray(c), mx_ref.live(s))
def emit(q):
    return q[0], q[1]
def packed(v, rng):
    q = [mx_ref.quantize(np.ascontiguousarray(v[r])) for r in range(N)]
    return np.stack([a for a, b in q]), np.stack([mx_ref.plane(b, rng) for a, b in q])
def values_of_codes():
    e, c = np.zeros((128, 128, 4), np.float32), np.zeros((128, 2, 4), np.uint8)
    e[np.arange(128), np.arange(128), 0] = 1
    c[:127, :, 0] = np.arange(256).reshape(2, 128).T[:127]
    return mx_ref.matmul(mx_ref.quantize(e.reshape(128, 512).astype(BF)), (c.reshape(128, 8), np.full((16, 2), 127, np.uint8))).T.reshape(-1).astype(np.float64)
CODE_VALUE, SCALE_VALUE = values_of_codes(), 2.0 ** (np.arange(256) - 127.0)
def decode(q):
    return (CODE_VALUE[q[0]].reshape(16, 8, -1, 4) * SCALE_VALUE[q[1]][:, None, :, None] + 0.0).reshape(128, -1).astype(np.float32)
def f(rng, *shape):
    return mx_ref.flush((rng.standard_normal(shape, dtype=np.float32) * np.exp2(rng.integers(-2, 3, shape[:-1] + (1,)))).astype(BF))
def wide(rng, *shape, cols=0):
    v = rng.standard_normal(shape, dtype=np.float32) * np.exp2(rng.integers(-12, 13, shape)).astype(np.float32)
    if cols: v *= np.repeat(np.exp2(rng.integers(-cols, cols + 1, shape[:-2] + (1, shape[-1] // 4))) * (rng.random(shape[:-2] + (1, shape[-1] // 4)) > 0.0625), 4, axis=-1).astype(np.float32)
    return mx_ref.flush(v.astype(BF))
C, HALF = 448, 224
STEP = [1, 2, 3]
def numbers_of(rng):
    return {"x": np.array(f(rng, N, 128, 4 * C)), "lv": np.array(f(rng, N, 128, 4 * C)), "u": np.array(f(rng, N, 128, 512)), "v": np.array(f(rng, N, 128, 512))}
def names(rng):
    return rng.permuted(np.tile(np.arange(2 * C), (N, 8, 1)), axis=2)
def paired(rng, roots):
    p, n = np.flatnonzero(roots), np.flatnonzero(~roots)
    k = np.zeros(2 * C, np.int64)
    k[p] = rng.permutation(n)
    k[np.concatenate([n, np.arange(C, 2 * C)])] = rng.permutation(np.concatenate([p, np.arange(C, 2 * C)]))
    return k
def stored(k):
    return {"lt": np.stack([gtable(k[r][:, :C]) for r in range(N)]), "rt": np.stack([gtable(k[r][:, C:]) for r in range(N)])}
def layers(rng):
    return np.array(f(rng, N, 128, 2048)).reshape(N, 8, 16, 4, 8, 16, 4)
def weights(rng, w):
    c, p = packed(np.ascontiguousarray(w).reshape(N, 128, 2048), rng)
    return {"wc": c, "ws": p}
def setup_inputs(rng):
    return {**numbers_of(rng), **stored(names(rng)), **weights(rng, layers(rng))}
def setup_inputs_ties(rng):
    d = numbers_of(rng)
    o = rng.permutation(N)
    k = rng.integers(-1, 2, (N, 8, 4, C)).astype(np.float32)
    k[o[1]] = 1
    e = names(rng)
    for g in range(8):
        p = rng.permutation(C) < HALF
        k[o[3], g, 0] = np.where(p, 1.0, -1.0)
        if g % 2:
            k[o[3], g, 1] = np.minimum(k[o[3], g, 1], 0)
            k[o[3], g, 2] = k[o[3], g, 0]
        e[o[3], g] = paired(rng, p)
    x = d["x"].reshape(N, 8, 16, C, 4)
    x[:, :, :8] = 0
    x[:, :, :4, :, 0] = k.astype(BF)
    c = np.ones(N, np.float32)
    c[o[0]] = 0
    c[o[2]] = -1
    u = d["u"].reshape(N, 128, 128, 4)
    for g in range(8):
        for h in range(16 * g, 16 * g + 4):
            u[:, :, h] = 0
            u[:, h, h, 0] = c.astype(BF)
    w = layers(rng)
    w[:, :, :, :, :, :8] = 0
    return {"x": x.reshape(N, 128, 4 * C), "lv": d["lv"], "u": u.reshape(N, 128, 512), "v": d["v"], **stored(e), **weights(rng, w)}
def setup_inputs_near(rng):
    d = numbers_of(rng)
    o = rng.permutation(N)
    t = int(np.flatnonzero(o == 0)[0])
    k = np.where(o % 2 == 0, 2.0 ** -30, 1.0).astype(np.float32)
    x = d["x"].astype(np.float32).reshape(N, 8, 16, C, 4)
    lv = d["lv"].astype(np.float32).reshape(N, 8, 16, C, 4)
    s = rng.integers(-1, 2, (N, 8, 4, C)) * np.where(o % 2 == 0, 2.0 ** -28, 1.0)[:, None, None, None]
    x[:, :, :8] = 0
    x[:, :, :4, :, 0] = 1.125 * s
    x[:, :, 4:8, :, 0] = -1.25 * s
    for r in range(N):
        at = [0, C - 1, int(rng.integers(C)), int(rng.integers(C))]
        for g, j in zip(rng.permutation(8)[:4], at): x[r, g, rng.integers(4), j, 0] = 2.0 ** 30 * rng.choice([-1.0, 1.0])
    x[t] = 0
    x[t, :, 7, :, 3] = 2.0 ** -29
    for z in (x, lv):
        z[:, :, 15, :, 3] = 4.0
        z[t, :, 8:] = rng.choice([-1.0, 1.0], (8, 8, C, 4)) * 2.0 ** -26
        z[t, :, 8:12, :, 0] *= np.float32(2.0 ** -4)
        z[t, ::2, 9:12:2, :, 0] = 2.0 ** -30
        z[t, :, 15, :, 3] = 2.0 ** -28
    u = d["u"].reshape(N, 128, 128, 4)
    w = layers(rng)
    w[:, :, :8] = 0
    w[:, :, :, :, :, :8] = 0
    w[:, :, :, 3, :, 15] = 0
    w[:, :, 15, 3, :, 15, 3] = 4.0
    w[t, :, 15, 3, :, 7, 3] = 4.0
    for g in range(8):
        for i in range(4):
            h = 16 * g + i
            u[:, :, h] = 0
            u[:, h, h, 0] = (1.125 * k).astype(BF)
            u[:, h + 4, h, 0] = k.astype(BF)
            u[t, :, h] = 0
            u[t, h, h, 1] = 1.125 * 2.0 ** -30
            u[t, h + 4, h, 1] = 2.0 ** -30
            w[t, g, 8 + i, 1, g, i, 0] = 1.125 * 2.0 ** -5
            w[t, g, 8 + i, 1, g, i + 4, 0] = -1.25 * 2.0 ** -5
    return {"x": x.reshape(N, 128, 4 * C).astype(BF), "lv": lv.reshape(N, 128, 4 * C).astype(BF), "u": u.reshape(N, 128, 512), "v": d["v"], **stored(names(rng)), **weights(rng, w)}
def setup_inputs_odd(rng):
    d = numbers_of(rng)
    x = np.zeros((N, 8, 16, C, 4), np.float32)
    lv = np.zeros((N, 8, 16, C, 4), np.float32)
    a = np.exp2(rng.integers(5, 9, (8, 1)).astype(np.float32))
    b = rng.integers(0, 2, (N, 8, 4, C))
    x[:, :, 0, :, 3] = 1.96875 * 2.0 ** 8
    x[:, :, 0:8:2, :, 0] = (8 + b) * 2.0 ** -8
    x[:, :, 1:8:2, :, 0] = (9 - b) * 2.0 ** -8
    for t in (x, lv):
        t[:, :, 7, :, 1] = 1.125 * a
        t[:, :, 7, :, 2] = 0.0703125 * a
    x[:, :, 9, :, 0] = -a
    u = d["u"].reshape(N, 128, 128, 4)
    w = np.zeros((N, 8, 16, 4, 8, 16, 4), np.float32)
    for g in range(8):
        w[:, g, 7, 0, g, 9, 1] = 28.0
        for i in range(4):
            u[:, :, 16 * g + i] = 0
            u[:, 16 * g + 2 * i, 16 * g + i, 0] = 1.0
            u[:, 16 * g + 2 * i + 1, 16 * g + i, 0] = -1.0
            w[:, g, 7, i, g, 10, 2] = [1.0, 1.25, 0.75, 0.5625][i] * 2.0 ** -5
    return {"x": x.reshape(N, 128, 4 * C).astype(BF), "lv": lv.reshape(N, 128, 4 * C).astype(BF), "u": u.reshape(N, 128, 512), "v": d["v"], **stored(names(rng)), **weights(rng, w.astype(BF))}
def setup_inputs_ends(rng):
    d = numbers_of(rng)
    n = np.arange(N)
    o = np.array([1, 0, 2, 3])[(n & 3) ^ rng.integers(0, 4, 2)[n >> 2]]
    x = np.zeros((N, 8, 16, C, 4), np.float32)
    lv = np.zeros((N, 8, 16, C, 4), np.float32)
    a = np.zeros((N, 8, 4))
    k = names(rng)
    w = np.zeros((N, 128, 4, 128, 4), np.float32)
    i, c = np.arange(128), np.arange(C)
    for r in range(N):
        a[r] = rng.choice([-1.0, 1.0], (8, 4)) * (rng.permutation(8) > 1)[:, None]
        roots = rng.permutation(C) < HALF
        s = rng.choice([-1.0, 1.0], (2, 8, 16, C, 4))
        size = (0.6 + 0.05 * rng.random((2, 8, 16, C, 4))) * 2.0 ** 30
        if o[r] == 0:
            s[:] = -1.0
            k[r] = np.concatenate([2 * C - 1 - c, C - 1 - c])
        if o[r] == 1:
            s[0] = np.where(roots, 1.0, -1.0)[None, None, :, None]
            for g in range(8): k[r, g] = paired(rng, ~roots if a[r, g, 0] < 0 else roots)
        if o[r] == 2: k[r] = np.concatenate([(c + 1) % C, 2 * C - 1 - c])
        if o[r] == 3:
            s[0] = s[0][:, :1, :, :1]
            size[:] = 2.0 ** -28
            for j, g in enumerate(rng.permutation(8)):
                k[r, g] = np.concatenate([rng.permutation(C) + C * (j % 2), rng.permutation(C) + C * (1 - j % 2)])
        x[r], lv[r] = s * size
        if o[r] == 2: w[r] = rng.choice([-1.0, 1.0], (128, 4, 128, 4)) * 2.0 ** -6
        else:
            for b in range(4): w[r, i, b, i, b] = -1.0 if o[r] < 2 else 64.0
    size = np.where(o == 3, 2.0 ** -30, 2.0 ** 30)
    u = d["u"].reshape(N, 128, 128, 4)
    for j in range(4): u[:, :, j::16] = (a[:, :, j] * size[:, None] + 0.0).astype(np.float32).astype(BF)[:, None, :, None]
    v = rng.choice([-1.0, 1.0], (N, 128, 512)) * size[:, None, None]
    return {"x": x.reshape(N, 128, 4 * C).astype(BF), "lv": lv.reshape(N, 128, 4 * C).astype(BF), "u": u.reshape(N, 128, 512), "v": v.astype(np.float32).astype(BF), **stored(k), **weights(rng, w.astype(BF))}
def setup_inputs_spread(rng):
    d = setup_inputs(rng)
    d["x"] = wide(rng, N, 128, 4 * C, cols=6)
    d["lv"] = wide(rng, N, 128, 4 * C, cols=6)
    return d
def check_inputs(d):
    b = []
    for k in ("x", "lv", "u", "v"):
        a = np.abs(d[k].astype(np.float32))
        if not (np.isfinite(a).all() and ((a == 0) | (a >= 2.0 ** -30) & (a <= 2.0 ** 30)).all()): b.append("a value of " + k)
    none, least, most = [emit(mx_ref.quantize(np.full((128, 16), k, np.float32).astype(BF)))[1][0, 0] for k in (0.0, 2.0 ** -6, 2.0 ** 6)]
    for r in range(N):
        if (np.sort(np.concatenate([gentries(d["lt"][r]), gentries(d["rt"][r])], axis=1), axis=1) != np.arange(2 * C)).any(): b.append("lt and rt: not every name once in a group")
        if ((d["wc"][r] == 0x7F) | (d["wc"][r] == 0xFF)).any(): b.append("wc: a code that is no number")
        s = mx_ref.live(d["ws"][r])
        if ((s != none) & ((s < least) | (s > most))).any(): b.append("ws: a scale out of range")
        if (((d["wc"][r].reshape(16, 8, 512, 4) & 0x7F) != 0) & (s == none)[:, None, :, None]).any(): b.append("wc: a code other than zero under the scale of zeros")
    return b
def rewrite(left, right, act, turn):
    g, c = np.nonzero((left < C) & (act > 0) & (np.take_along_axis(act, left % C, 1) < 0))
    s = left[g, c]
    a, b, z = left[g, s], right[g, s], right[g, c]
    t = turn[g, a % C] > 0
    left, right = left.copy(), right.copy()
    left[g, c], right[g, c] = np.where(t, a, s), np.where(t, s, b)
    left[g, s], right[g, s] = np.where(t, b, a), z
    return left, right
def reference(x, lv, u, v, lt, rt, wc, ws):
    qu = [mx_ref.quantize(u[r]) for r in range(N)]
    lay = [pk(wc[r], ws[r]) for r in range(N)]
    left, right = [gentries(lt[r]) for r in range(N)], [gentries(rt[r]) for r in range(N)]
    now, leaf = [x[r] for r in range(N)], [lv[r] for r in range(N)]
    for step in STEP:
        made = []
        for r in range(N):
            s = mx_ref.matmul(qu[r], mx_ref.quantize(now[r])).reshape(8, 16, C)
            for j in range(2): left[r], right[r] = rewrite(left[r], right[r], s[:, 2 * j], s[:, 2 * j + 1])
            win = np.concatenate([now[r], leaf[r]], axis=1)
            z = mx_ref.quantize(((gcols(win, left[r]).astype(np.float32) + gcols(win, right[r]).astype(np.float32)) * np.float32(0.5)).astype(BF))
            made.append(tile([mx_ref.matmul(pick(lay[r], np.arange(128 * b, 128 * b + 128)), z) * np.float32(0.03125) for b in range(4)]))
        for r in range(N):
            p = r ^ step
            m = np.take_along_axis(left[p], right[r] % C, 1) % C
            far = gcols(decode(mx_ref.quantize(made[p])).astype(BF), m[:, :HALF])
            leaf[r] = np.concatenate([far, gcols(made[r], m[:, HALF:])], axis=1)
            now[r] = (now[r].astype(np.float32) + leaf[r].astype(np.float32)).astype(BF)
    y, gr = np.zeros((N, 128, C), np.float32), np.zeros((N, 8, 2 * C), np.float32)
    oc, osc = np.zeros((N, 128, 4 * C), np.uint8), np.zeros((N, 16, C), np.uint8)
    for r in range(N):
        q = mx_ref.quantize(now[r])
        y[r] = mx_ref.matmul(mx_ref.quantize(v[r]), q)
        gr[r] = np.concatenate([left[r], right[r]], axis=1)
        oc[r], osc[r] = emit(q)
    return {"y": y, "gr": gr, "oc": oc, "osc": osc}

@@ -1,0 +1,417 @@
+from concourse.mybir import dt, AluOpType, ActivationFunctionType
+
+ROUNDS = [1, 2, 3]
+ADD, SUB, MUL = AluOpType.add, AluOpType.subtract, AluOpType.mult
+GE, GT, LT = AluOpType.is_ge, AluOpType.is_gt, AluOpType.is_lt
+NE, ANDB, SHR = AluOpType.not_equal, AluOpType.bitwise_and, AluOpType.arith_shift_right
+COPY = ActivationFunctionType.Copy
+F32, BF, I32, U16, U8, MXC = "float32", "bfloat16", "int32", "uint16", "uint8", "float8_e4m3fn_x4"
+
+
+def _sb(n, d):
+    return ("sbuf", [128, n], d)
+
+
+SCRATCH = {
+    "xa": _sb(1792, BF), "xb": _sb(1792, BF), "lvt": _sb(1792, BF), "ut": _sb(512, BF), "vt": _sb(512, BF),
+    "one": _sb(512, BF), "et": _sb(2048, BF), "win": _sb(4 * 896, BF), "zr": _sb(1792, BF), "zt": _sb(1792, BF),
+    "hw": _sb(1792, BF), "sh": _sb(896, BF), "yb": _sb(448, F32),
+    "qu": _sb(128, MXC), "su": _sb(128, U8), "qk": _sb(128, MXC), "sk": _sb(128, U8), "qv": _sb(128, MXC), "sv": _sb(128, U8),
+    "qe": _sb(512, MXC), "se": _sb(512, U8), "qw": _sb(512, MXC), "sw": _sb(512, U8), "qx": _sb(448, MXC), "sx": _sb(448, U8),
+    "qz": _sb(448, MXC), "sz": _sb(448, U8),
+    "lti": _sb(28, I32), "rti": _sb(28, I32), "pi": _sb(1, I32), "ci": _sb(28, I32), "ui": _sb(8, I32), "ki": _sb(7, I32),
+    "kf": _sb(7, F32), "kt": _sb(16, F32), "cl2": _sb(4, U16), "cl1": _sb(2, U16), "clu": _sb(8, U16),
+    "tb0": _sb(448, F32), "tt": _sb(1792, F32), "tg": _sb(1792, BF), "tg2": _sb(448, BF), "ta": _sb(448, F32), "tp": _sb(448, F32),
+    "tm": _sb(448, F32), "ls": _sb(896, F32), "wq": _sb(896, F32), "sg": _sb(912, BF), "gg1": _sb(896, BF), "gg2": _sb(448, BF),
+    "gg3": _sb(448, BF), "h1": _sb(896, F32), "h2": _sb(448, BF), "p0": _sb(896, F32), "p1": _sb(896, F32), "a1": _sb(448, F32),
+    "ms": _sb(448, F32), "cw": _sb(160, F32), "xx": _sb(96, F32), "cw1": _sb(96, F32), "xy": _sb(64, F32),
+    "nl": _sb(64, U16), "nl1": _sb(64, U16), "nf": _sb(64, F32), "pw": _sb(32, U16),
+    "t28": _sb(28, F32), "ff": _sb(112, F32), "pr": _sb(112, F32), "p3": _sb(28, F32), "uu": _sb(56, F32),
+    "dl0": _sb(112, F32), "dl1": _sb(112, F32), "d30": _sb(28, F32), "d31": _sb(28, F32),
+    "ps": ("psum", [128, 4096], F32),
+}
+for _k in range(3):
+    SCRATCH.update({"rc%d" % _k: _sb(64, U16), "mu%d" % _k: _sb(32, U16), "lr%d" % _k: _sb(28, U16), "lm%d" % _k: _sb(14, U16),
+                    "qs%d" % _k: _sb(224, MXC), "ss%d" % _k: _sb(224, U8), "ql%d" % _k: _sb(224, MXC), "sl%d" % _k: _sb(224, U8)})
+ENG_SEM = {"v": "eV", "s": "eS", "t": "eT", "p": "eP"}
+SEMAPHORES = list(ENG_SEM.values()) + ["loc"] + ["d%d" % i for i in range(32)] + ["%s%d" % (a, k) for a in ("aR", "aM", "aC", "aS") for k in range(3)]
+
+
+def rank_program(g, core, T, topo):
+    rank = T.rank_of(core)
+    if rank is None:
+        return
+    eng = {"v": g.vector, "s": g.scalar, "t": g.tensor, "p": g, "y": g.sync}
+    cnt = {"v": 0, "s": 0, "t": 0, "p": 0}
+    know = {q: {} for q in eng}
+    snap, recs, ndma, nloc = {}, {}, [0], [0]
+
+    def wait(q, sem, val):
+        if know[q].get(sem, 0) >= val:
+            return
+        eng[q].wait_ge(T.sem[sem], val)
+        for s, n in snap.get((sem, val), {}).items():
+            know[q][s] = max(know[q].get(s, 0), n)
+        know[q][sem] = max(know[q].get(sem, 0), val)
+
+    def need(q, src, reads, writes):
+        w = {}
+        for acc, wr in [(a, False) for a in reads] + [(a, True) for a in writes]:
+            name, cols = acc
+            for rn, rcols, rwr, rsrc, sem, val in recs.get(name, []):
+                if name == "ps":
+                    if rsrc == src or not (cols & rcols):
+                        continue
+                elif not (wr or rwr) or not (cols & rcols):
+                    continue
+                elif rsrc == src and not rwr:
+                    continue
+                w[sem] = max(w.get(sem, 0), val)
+        for sem in sorted(w):
+            wait(q, sem, w[sem])
+
+    def note(src, sem, val, reads, writes):
+        for name, cols in writes:
+            recs[name] = [r for r in recs.get(name, []) if not (r[1] <= cols)]
+        for name, cols in reads:
+            recs[name] = [r for r in recs.get(name, []) if not (not r[2] and r[3] == src and src != "dma" and r[1] <= cols)]
+        for acc, wr in [(a, False) for a in reads] + [(a, True) for a in writes]:
+            recs.setdefault(acc[0], []).append((acc[0], acc[1], wr, src, sem, val))
+
+    def acc(*views):
+        out = []
+        for v in views:
+            for name, cols in v[1]:
+                if name == "ps":
+                    cols = frozenset(x // 512 for x in cols)
+                out.append((name, frozenset(cols)))
+        return out
+
+    def V(name, a, b, s=1):
+        return (T[name][:, a:b] if s == 1 else T[name][:, a:b:s], [(name, range(a, b, s))])
+
+    def I(name, a, b, off, c, d):
+        return (T[name][:, a:b].indirect(T[off][:, c:d]), [(name, range(a, b)), (off, range(c, d))])
+
+    def do(q, call, out, *ins):
+        outs = list(out) if isinstance(out, list) else [out]
+        reads, writes = [], acc(*[(o[0], o[1][:1]) for o in outs])
+        for o in outs:
+            reads += acc((None, o[1][1:]))
+        reads += acc(*ins)
+        need(q, q, reads, writes)
+        r = call(eng[q])
+        cnt[q] += 1
+        sem = ENG_SEM[q]
+        r.then_inc(T.sem[sem], 1)
+        k = dict(know[q])
+        k[sem] = cnt[q]
+        snap[(sem, cnt[q])] = k
+        note(q, sem, cnt[q], reads, writes)
+
+    def dma(q, out_ap, in_ap, reads=(), writes=()):
+        need(q, "dma", acc((None, reads)), acc((None, writes)))
+        sem = "d%d" % ndma[0]
+        ndma[0] += 1
+        eng[q].dma_start(out_ap, in_ap).then_inc(T.sem[sem], 16)
+        snap[(sem, 16)] = dict(know[q])
+        note("dma", sem, 16, acc((None, reads)), acc((None, writes)))
+
+    def send(dst, out_ap, in_ap, sem, view):
+        need("p", "rem", acc(view), [])
+        a = topo.addr(dst)
+        g.remote_dma(out_ap, in_ap, T.sem[sem], T.sem["loc"], a[1], a[0], topo.mask(core, dst))
+        nloc[0] += len(topo.engines(core, dst))
+
+    def lands(name, n, sem, src):
+        recs.setdefault(name, []).append((name, frozenset(range(n)), True, "rem", sem, len(topo.engines(src, core))))
+
+    def tt(out, a, b, op):
+        do("v", lambda e: e.tensor_tensor(out[0], a[0], b[0], op), out, a, b)
+
+    def ts(out, a, s1, s2, op0, *op1):
+        sc = [x for x in (s1, s2) if isinstance(x, tuple)]
+        do("v", lambda e: e.tensor_scalar(out[0], a[0], s1[0] if isinstance(s1, tuple) else s1, s2[0] if isinstance(s2, tuple) else s2, op0, *op1), out, a, *sc)
+
+    def cp(out, a):
+        do("v", lambda e: e.tensor_copy(out[0], a[0]), out, a)
+
+    def tr(out, a):
+        do("v", lambda e: e.transpose(out[0], a[0]), out, a)
+
+    def fill(out, c):
+        do("v", lambda e: e.memset(out[0], c), out)
+
+    def act(out, a, func=COPY, scale=1.0):
+        if isinstance(scale, tuple):
+            do("s", lambda e: e.activation(out[0], a[0], func, scale=scale[0]), out, a, scale)
+        else:
+            do("s", lambda e: e.activation(out[0], a[0], func, scale=scale), out, a)
+
+    def quant(q, s, a, b, tile, ta, tb):
+        do("v", lambda e: e.quantize_mx(T[q][:, a:b], T[s][:, a:b], T[tile][:, ta:tb]), [V(q, a, b), V(s, a, b)], V(tile, ta, tb))
+
+    def mm(bank, n, ql, sl, la, qr, sr, a, b):
+        o = V("ps", 512 * bank, 512 * bank + n)
+        do("t", lambda e: e.matmul_mx(o[0], T[ql][:, la:la + 128], T[sl][:, la:la + 128], T[qr][:, a:b], T[sr][:, a:b], True, True), o,
+           V(ql, la, la + 128), V(sl, la, la + 128), V(qr, a, b), V(sr, a, b))
+
+    def PS(bank, n):
+        return V("ps", 512 * bank, 512 * bank + n)
+
+    def conv2(out):
+        tr(V("xx", 16, 80), V("cw", 0, 64))
+        tr(V("cw", 64, 160), V("xx", 0, 96))
+        cp(out, I("cw", 0, 160, "cl2", 0, 4))
+
+    def conv1(out):
+        tr(V("xy", 16, 48), V("cw1", 0, 32))
+        tr(V("cw1", 32, 96), V("xy", 0, 64))
+        cp(out, I("cw1", 0, 96, "cl1", 0, 2))
+
+    def rewrite(plus, minus, turns, base, nxt, dl, d3):
+        tt(V("ff", 1, 112, 2), plus, minus, MUL)
+        for o, i, a in turns:
+            tt(o, i, a, MUL)
+        tt(V("pr", 0, 112), V("ff", 0, 112), V(dl, 0, 112), MUL)
+        tt(V("p3", 0, 28), V("ff", 0, 56, 2), V(d3, 0, 28), MUL)
+        tt(V("uu", 0, 56), V("pr", 0, 56), V("pr", 56, 112), ADD)
+        tt(V("uu", 1, 56, 2), V("uu", 1, 56, 2), V("p3", 0, 28), ADD)
+        tt(V("cw", 0, 56), base, V("uu", 0, 56), ADD)
+        return lambda: cp(nxt, V("cw", 0, 56))
+
+    L0, R0, LR0 = V("tb0", 5, 448, 16), V("tb0", 13, 448, 16), V("tb0", 5, 448, 8)
+    L1, R1, LR1 = V("tt", 901, 1344, 16), V("tt", 909, 1344, 16), V("tt", 901, 1344, 8)
+
+    def ahead_lists():
+        tr(V("tp", 0, 448), V("p0", 0, 448))
+        ts(V("cw1", 0, 28), V("tp", 4, 448, 16), 896.0, None, ADD)
+        conv1(V("pw", 0, 32))
+        tt(V("dl0", 56, 112, 2), R0, L0, SUB)
+        tt(V("dl0", 57, 112, 2), V("tp", 13, 448, 16), R0, SUB)
+
+    def scores(half):
+        a = 224 * half
+        mm(4 + half, 224, "qk", "sk", 0, "qx", "sx", a, a + 224)
+        ts(V("sg", a, a + 224), PS(4 + half, 224), V("kf", 6, 7), 0.0, MUL, GT)
+        tr(V("tg", 896 + a, 1120 + a), V("sg", a, a + 224))
+
+    def for_leaves(half):
+        a = 224 * half
+        act(V("sg", 448 + a, 672 + a), V("sg", a, a + 224), COPY, V("kf", 5, 6))
+
+    dma("y", T.lti[:, 0:28], T.lt[:, :], writes=[("lti", range(28))])
+    dma("s", T.rti[:, 0:28], T.rt[:, :], writes=[("rti", range(28))])
+    dma("s", T.ut[:, :], T.u[:, :], writes=[("ut", range(512))])
+    for h in range(2):
+        dma("y", T.xa[:, 896 * h:896 * h + 896], T.x[:, 896 * h:896 * h + 896], writes=[("xa", range(896 * h, 896 * h + 896))])
+    dma("s", T.lvt[:, :], T.lv[:, :], writes=[("lvt", range(1792))])
+    dma("y", T.qw[:, 0:512].bitcast(dt.uint8), T.wc[:, :], writes=[("qw", range(512))])
+    dma("y", T.sw[:, 0:512], T.ws[:, :], writes=[("sw", range(512))])
+    dma("y", T.vt[:, :], T.v[:, :], writes=[("vt", range(512))])
+    for k in range(3):
+        p = T.cores[rank ^ ROUNDS[k]]
+        lands("lr%d" % k, 28, "aR%d" % k, p)
+        lands("lm%d" % k, 14, "aM%d" % k, p)
+        lands("ql%d" % k, 224, "aC%d" % k, p)
+        lands("sl%d" % k, 224, "aS%d" % k, p)
+    do("p", lambda e: e.iota(T.pi[:, 0:1], [[0, 1]], 0, 1), V("pi", 0, 1))
+    do("p", lambda e: e.iota(T.ci[:, 0:28], [[32, 14], [0, 2]], -896, 0), V("ci", 0, 28))
+    do("p", lambda e: e.iota(T.ui[:, 0:8], [[16, 8]], 0, 0), V("ui", 0, 8))
+    fill(V("one", 0, 512), 1.0)
+    for b in range(4):
+        do("p", lambda e: e.affine_select(T.et[:, 512 * b:512 * b + 512], T.one[:, 0:512], [[-1, 512]], AluOpType.is_equal, 0.0, b, 4),
+           V("et", 512 * b, 512 * b + 512), V("one", 0, 512))
+    fill(V("tb0", 0, 448), 0.0)
+    for name, a, b in (("p0", 0, 448), ("gg1", 448, 896), ("h1", 448, 896), ("p1", 0, 448)):
+        act(V(name, a, b), V("tb0", 0, 448), COPY, 0.0)
+    for i, (s1, s2, ops) in enumerate([(15, None, (ANDB,)), (4, 1, (SHR, ANDB)), (1, None, (ANDB,)), (31, None, (ANDB,)), (3, None, (ANDB,)), (4, None, (ANDB,))]):
+        ts(V("ki", i, i + 1), V("pi", 0, 1), s1, s2, *ops)
+    fill(V("cw", 0, 64), 0.0)
+    fill(V("xx", 0, 96), 0.0)
+    cp(V("kf", 0, 6), V("ki", 0, 6))
+
+    def K(i):
+        return V("kt", i, i + 1)
+    X_, H_, B_ = V("kf", 0, 1), V("kf", 1, 2), V("kf", 2, 3)
+    tt(K(0), B_, H_, SUB)
+    ts(K(2), H_, -32.0, 98.0, MUL, ADD)
+    ts(K(4), B_, 2.0, -33.0, MUL, ADD)
+    tt(K(1), K(0), K(0), MUL)
+    ts(K(3), B_, -4.0, K(2), MUL, ADD)
+    tt(K(4), K(4), K(3), ADD)
+    tt(K(3), K(3), K(1), MUL)
+    tt(K(4), K(4), K(1), MUL)
+    ts(K(3), X_, 2.0, K(3), MUL, ADD)
+    tt(K(4), K(4), X_, ADD)
+    ts(V("clu", 0, 8), V("ui", 0, 8), V("kf", 4, 5), None, ADD)
+    for k, c in enumerate([0.0, 32.0, 1.0, 33.0]):
+        ts(V("cl2", k, k + 1), K(3), c, None, ADD)
+    for k in range(2):
+        ts(V("cl1", k, k + 1), K(4), 16.0 * k, None, ADD)
+    ts(V("kf", 6, 7), V("kf", 5, 6), -0.5, 1.0, MUL, ADD)
+    ts(V("kf", 5, 6), V("kf", 5, 6), -0.25, 1.0, MUL, ADD)
+    ts(V("tb0", 4, 448, 16), V("ci", 0, 28), V("kf", 3, 4), None, ADD)
+    fill(V("sg", 896, 912), 0.0)
+    fill(V("cw1", 0, 32), 0.0)
+    fill(V("xy", 0, 64), 0.0)
+    cp(V("cw", 0, 56, 2), V("lti", 0, 28))
+    cp(V("cw", 1, 56, 2), V("rti", 0, 28))
+    cp(V("nl", 0, 28), V("lti", 0, 28))
+    cp(V("nl", 32, 60), V("rti", 0, 28))
+    conv2(V("nf", 0, 64))
+    cp(L0, V("nf", 0, 28))
+    cp(R0, V("nf", 32, 60))
+    tr(V("ls", 0, 448), V("tb0", 0, 448))
+    act(V("ls", 448, 896), V("ls", 0, 448))
+    act(V("a1", 0, 448), I("ls", 0, 896, "nl", 0, 28))
+    quant("qu", "su", 0, 128, "ut", 0, 512)
+    do("v", lambda e: e.tensor_copy(T.qk[:, 0:128].bitcast(dt.uint32), T.qu[:, 0:128].bitcast(dt.uint32).indirect(T.clu[:, 0:8])),
+       V("qk", 0, 128), V("qu", 0, 128), V("clu", 0, 8))
+    do("v", lambda e: e.tensor_copy(T.sk[:, 0:128], T.su[:, 0:128].indirect(T.clu[:, 0:8])), V("sk", 0, 128), V("su", 0, 128), V("clu", 0, 8))
+    cp(I("p0", 0, 896, "nl", 0, 28), V("ls", 0, 448))
+    for h in range(2):
+        quant("qx", "sx", 224 * h, 224 * h + 224, "xa", 896 * h, 896 * h + 896)
+    for h in range(2):
+        scores(h)
+        for_leaves(h)
+    ahead_lists()
+    tr(V("ta", 0, 448), V("a1", 0, 448))
+
+    xs, nl = ["xa", "xb"], "nl"
+    for k in range(3):
+        last = k == 2
+        p = T.cores[rank ^ ROUNDS[k]]
+        old, new = xs[k % 2], xs[(k + 1) % 2]
+        act(V("gg1", 0, 448), I("sg", 0, 896, nl, 0, 28))
+        cp(V("gg3", 0, 448), I("sg", 0, 912, "pw", 0, 28))
+        act(V("gg2", 0, 448), I("gg1", 0, 896, nl, 0, 28))
+        tr(V("tg", 448, 896), V("gg1", 0, 448))
+        tr(V("tg", 1344, 1792), V("gg3", 0, 448))
+        tt(V("dl0", 0, 56), V("ta", 5, 448, 8), LR0, SUB)
+        tt(V("d30", 0, 28), L0, V("ta", 13, 448, 16), SUB)
+        tr(V("tg", 0, 448), V("gg2", 0, 448))
+        act(V("tt", 896, 1344), V("tg", 896, 1344))
+        if k == 0:
+            for b in range(4):
+                act(V("win", 896 * b, 896 * b + 448), V("xa", b, 1792, 4), COPY, 0.5)
+        else:
+            for b in range(4):
+                act(V("win", 896 * b, 896 * b + 224), V(old, b, 896, 4), COPY, 0.5)
+        put = rewrite(V("tg", 896, 1792, 16), V("tg", 452, 1344, 16), [(V("ff", 0, 112, 2), V("ff", 1, 112, 2), V("tg", 1, 896, 16))],
+                      LR0, LR1, "dl0", "d30")
+        put()
+        tr(V("wq", 0, 448), V("tt", 896, 1344))
+        act(V("wq", 448, 896), V("wq", 0, 448), COPY, V("kf", 5, 6))
+        conv2(V("nl1", 0, 64))
+        act(V("h1", 0, 448), I("wq", 0, 896, "nl1", 0, 28))
+        act(V("h2", 0, 448), I("h1", 0, 896, "nl1", 0, 28))
+        cp(I("p1", 0, 896, "nl1", 0, 28), V("wq", 0, 448))
+        if k == 0:
+            for b in range(4):
+                act(V("win", 896 * b + 448, 896 * b + 896), V("lvt", b, 1792, 4), COPY, 0.5)
+        else:
+            for b in range(4):
+                act(V("win", 896 * b + 448, 896 * b + 672), PS(b, 224), COPY, 0.5)
+        if not last:
+            act(V("p0", 0, 448), V("wq", 0, 448), COPY, 0.0)
+        tt(V("dl1", 56, 112, 2), R1, L1, SUB)
+        tr(V("tt", 448, 896), V("h1", 0, 448))
+        tt(V("dl1", 0, 56), V("tt", 453, 896, 8), LR1, SUB)
+        tt(V("d31", 0, 28), L1, V("tt", 461, 896, 16), SUB)
+        tr(V("tg2", 0, 448), V("h2", 0, 448))
+        tr(V("tt", 1344, 1792), V("p1", 0, 448))
+        tt(V("dl1", 57, 112, 2), V("tt", 1357, 1792, 16), R1, SUB)
+        put = rewrite(V("tt", 898, 1792, 16), V("tt", 454, 1344, 16),
+                      [(V("ff", 0, 56, 2), V("ff", 1, 56, 2), V("tg2", 3, 448, 16)), (V("ff", 56, 112, 2), V("ff", 57, 112, 2), V("tt", 451, 896, 16))],
+                      LR1, LR0, "dl1", "d31")
+        nl = "rc%d" % k
+        conv2(V(nl, 0, 64))
+        send(p, T["lr%d" % k][:, 0:28], T[nl][:, 32:60], "aR%d" % k, V(nl, 32, 60))
+        put()
+        tr(V("ls", 0, 448), V("tb0", 0, 448))
+        for h in range(2):
+            for b in range(4):
+                act(V("zr", 448 * b + 224 * h, 448 * b + 224 * h + 224), I("win", 896 * b, 896 * b + 896, nl, 32 + 14 * h, 46 + 14 * h))
+            if h == 0:
+                act(V("ls", 448, 896), V("ls", 0, 448))
+        for h in range(2):
+            for b in range(4):
+                o, w = V("zt", 896 * h + b, 896 * h + 896, 4), I("win", 896 * b, 896 * b + 896, nl, 14 * h, 14 * h + 14)
+                tt(o, w, V("zr", 448 * b + 224 * h, 448 * b + 224 * h + 224), ADD)
+            quant("qz", "sz", 224 * h, 224 * h + 224, "zt", 896 * h, 896 * h + 896)
+            for b in range(4):
+                mm(4 * h + b, 224, "qw", "sw", 128 * b, "qz", "sz", 224 * h, 224 * h + 224)
+        if last:
+            for i, q in enumerate((5, 13)):
+                dma("y", T.gr[:, 448 * i:448 * i + 448], T.ls[q:128:16, 0:448], reads=[("ls", range(448))])
+        act(V("ms", 0, 448), I("ls", 0, 896, "lr%d" % k, 0, 28))
+        tr(V("tm", 0, 448), V("ms", 0, 448))
+        ts(V("t28", 0, 28), V("tm", 5, 448, 16), 448.0, -448.0, GE, MUL)
+        tt(V("cw1", 0, 28), V("tm", 5, 448, 16), V("t28", 0, 28), ADD)
+        mu, lm = "mu%d" % k, "lm%d" % k
+        conv1(V(mu, 0, 32))
+        send(p, T[lm][:, 0:14], T[mu][:, 14:28], "aM%d" % k, V(mu, 14, 28))
+        for h in range(2):
+            for b in range(4):
+                o, i = V("hw", 448 * b + 224 * h, 448 * b + 224 * h + 224), PS(4 * h + b, 224)
+                if h == 0 or b % 2:
+                    act(o, i, COPY, 0.03125)
+                else:
+                    ts(o, i, 0.03125, None, MUL)
+        for b in range(4):
+            o, w = V("sh", b, 896, 4), I("hw", 448 * b, 448 * b + 448, mu, 0, 14)
+            if b % 2:
+                act(o, w)
+            else:
+                cp(o, w)
+        qs, ss, ql, sl = "qs%d" % k, "ss%d" % k, "ql%d" % k, "sl%d" % k
+        quant(qs, ss, 0, 224, "sh", 0, 896)
+        send(p, T[ql][:, 0:224].bitcast(dt.uint8), T[qs][:, 0:224].bitcast(dt.uint8), "aC%d" % k, V(qs, 0, 224))
+        send(p, T[sl][:, 0:224], T[ss][:, 0:224], "aS%d" % k, V(ss, 0, 224))
+        if not last:
+            cp(I("p0", 0, 896, nl, 0, 28), V("ls", 0, 448))
+            act(V("a1", 0, 448), I("ls", 0, 896, nl, 0, 28))
+        for b in range(4):
+            tt(V(new, 896 + b, 1792, 4), I("hw", 448 * b, 448 * b + 448, lm, 0, 14), V(old, 896 + b, 1792, 4), ADD)
+        quant("qx", "sx", 224, 448, new, 896, 1792)
+        if k == 0:
+            quant("qe", "se", 0, 512, "et", 0, 2048)
+            quant("qv", "sv", 0, 128, "vt", 0, 512)
+        if not last:
+            scores(1)
+            ahead_lists()
+            for b in range(4):
+                act(V("win", 896 * b + 672, 896 * b + 896), I("hw", 448 * b, 448 * b + 448, lm, 0, 14), COPY, 0.5)
+            for b in range(4):
+                act(V("win", 896 * b + 224, 896 * b + 448), V(new, 896 + b, 1792, 4), COPY, 0.5)
+            for_leaves(1)
+            act(V("p1", 0, 448), V("ls", 0, 448), COPY, 0.0)
+        else:
+            finish(mm, act, dma, V, PS, T, 1)
+        for b in range(4):
+            mm(b, 224, "qe", "se", 128 * b, ql, sl, 0, 224)
+        for b in range(4):
+            tt(V(new, b, 896, 4), V(old, b, 896, 4), PS(b, 224), ADD)
+        quant("qx", "sx", 0, 224, new, 0, 896)
+        if not last:
+            tr(V("ta", 0, 448), V("a1", 0, 448))
+            scores(0)
+            for_leaves(0)
+        else:
+            finish(mm, act, dma, V, PS, T, 0)
+    for q in "vstp":
+        wait("y", ENG_SEM[q], cnt[q])
+    for i in range(ndma[0]):
+        wait("y", "d%d" % i, 16)
+    g.wait_ge(T.sem["loc"], nloc[0])
+
+
+def finish(mm, act, dma, V, PS, T, half):
+    a, b = 224 * half, 224 * half + 224
+    mm(4 + half, 224, "qv", "sv", 0, "qx", "sx", a, b)
+    dma("y", T.oc[:, 4 * a:4 * b], T.qx[:, a:b].bitcast(dt.uint8), reads=[("qx", range(a, b))])
+    for k in range(4):
+        dma("y", T.osc[4 * k:4 * k + 4, a:b], T.sx[32 * k:32 * k + 4, a:b], reads=[("sx", range(a, b))])
+    act(V("yb", a, b), PS(4 + half, 224))
+    dma("s", T.y[:, a:b], T.yb[:, a:b], reads=[("yb", range(a, b))])

@@ -1,10 +1,11 @@
 from concourse.mybir import dt, AluOpType, ActivationFunctionType
 
 ROUNDS = [1, 2, 3]
+PARTS = [(0, 256), (256, 448)]
 ADD, SUB, MUL = AluOpType.add, AluOpType.subtract, AluOpType.mult
 GE, GT, LT = AluOpType.is_ge, AluOpType.is_gt, AluOpType.is_lt
 NE, ANDB, SHR = AluOpType.not_equal, AluOpType.bitwise_and, AluOpType.arith_shift_right
-COPY = ActivationFunctionType.Copy
+COPY, RELU, SIGN, MAX = ActivationFunctionType.Copy, ActivationFunctionType.Relu, ActivationFunctionType.Sign, AluOpType.max
 F32, BF, I32, U16, U8, MXC = "float32", "bfloat16", "int32", "uint16", "uint8", "float8_e4m3fn_x4"
 
 
@@ -21,10 +22,10 @@ SCRATCH = {
     "qz": _sb(448, MXC), "sz": _sb(448, U8),
     "lti": _sb(28, I32), "rti": _sb(28, I32), "pi": _sb(1, I32), "ci": _sb(28, I32), "ui": _sb(8, I32), "ki": _sb(7, I32),
     "kf": _sb(7, F32), "kt": _sb(16, F32), "cl2": _sb(4, U16), "cl1": _sb(2, U16), "clu": _sb(8, U16),
-    "tb0": _sb(448, F32), "tt": _sb(1792, F32), "tg": _sb(1792, BF), "tg2": _sb(448, BF), "ta": _sb(448, F32), "tp": _sb(448, F32),
+    "tb0": _sb(992, F32), "tt": _sb(1888, F32), "k1": _sb(4, F32), "k2": _sb(4, F32), "tg": _sb(1792, BF), "tg2": _sb(448, BF), "ta": _sb(448, F32), "tp": _sb(448, F32),
     "tm": _sb(448, F32), "ls": _sb(896, F32), "wq": _sb(896, F32), "sg": _sb(912, BF), "gg1": _sb(896, BF), "gg2": _sb(448, BF),
     "gg3": _sb(448, BF), "h1": _sb(896, F32), "h2": _sb(448, BF), "p0": _sb(896, F32), "p1": _sb(896, F32), "a1": _sb(448, F32),
-    "ms": _sb(448, F32), "cw": _sb(160, F32), "xx": _sb(96, F32), "cw1": _sb(96, F32), "xy": _sb(64, F32),
+    "ms": _sb(448, F32), "xx": _sb(96, F32), "cw1": _sb(96, F32), "xy": _sb(64, F32),
     "nl": _sb(64, U16), "nl1": _sb(64, U16), "nf": _sb(64, F32), "pw": _sb(32, U16),
     "t28": _sb(28, F32), "ff": _sb(112, F32), "pr": _sb(112, F32), "p3": _sb(28, F32), "uu": _sb(56, F32),
     "dl0": _sb(112, F32), "dl1": _sb(112, F32), "d30": _sb(28, F32), "d31": _sb(28, F32),
@@ -159,26 +160,25 @@ def rank_program(g, core, T, topo):
     def PS(bank, n):
         return V("ps", 512 * bank, 512 * bank + n)
 
-    def conv2(out):
-        tr(V("xx", 16, 80), V("cw", 0, 64))
-        tr(V("cw", 64, 160), V("xx", 0, 96))
-        cp(out, I("cw", 0, 160, "cl2", 0, 4))
+    def conv2(buf, o, out):
+        tr(V("xx", 16, 80), V(buf, o + 5, o + 510, 8))
+        tr(V(buf, o + 896, o + 992), V("xx", 0, 96))
+        cp(out, I(buf, o, o + 992, "cl2", 0, 4))
 
     def conv1(out):
         tr(V("xy", 16, 48), V("cw1", 0, 32))
         tr(V("cw1", 32, 96), V("xy", 0, 64))
         cp(out, I("cw1", 0, 96, "cl1", 0, 2))
 
-    def rewrite(plus, minus, turns, base, nxt, dl, d3):
-        tt(V("ff", 1, 112, 2), plus, minus, MUL)
+    def rewrite(plus, minus, acting, turns, base, nxt, dl, d3):
+        tt(V("ff", 1, 112, 2), plus, minus, acting)
         for o, i, a in turns:
             tt(o, i, a, MUL)
         tt(V("pr", 0, 112), V("ff", 0, 112), V(dl, 0, 112), MUL)
         tt(V("p3", 0, 28), V("ff", 0, 56, 2), V(d3, 0, 28), MUL)
         tt(V("uu", 0, 56), V("pr", 0, 56), V("pr", 56, 112), ADD)
         tt(V("uu", 1, 56, 2), V("uu", 1, 56, 2), V("p3", 0, 28), ADD)
-        tt(V("cw", 0, 56), base, V("uu", 0, 56), ADD)
-        return lambda: cp(nxt, V("cw", 0, 56))
+        tt(nxt, base, V("uu", 0, 56), ADD)
 
     L0, R0, LR0 = V("tb0", 5, 448, 16), V("tb0", 13, 448, 16), V("tb0", 5, 448, 8)
     L1, R1, LR1 = V("tt", 901, 1344, 16), V("tt", 909, 1344, 16), V("tt", 901, 1344, 8)
@@ -190,15 +190,23 @@ def rank_program(g, core, T, topo):
         tt(V("dl0", 56, 112, 2), R0, L0, SUB)
         tt(V("dl0", 57, 112, 2), V("tp", 13, 448, 16), R0, SUB)
 
+    def ahead_children():
+        tr(V("ta", 0, 448), V("a1", 0, 448))
+        tt(V("dl0", 0, 56), V("ta", 5, 448, 8), LR0, SUB)
+        tt(V("d30", 0, 28), L0, V("ta", 13, 448, 16), SUB)
+
     def scores(half):
         a = 224 * half
         mm(4 + half, 224, "qk", "sk", 0, "qx", "sx", a, a + 224)
-        ts(V("sg", a, a + 224), PS(4 + half, 224), V("kf", 6, 7), 0.0, MUL, GT)
-        tr(V("tg", 896 + a, 1120 + a), V("sg", a, a + 224))
 
-    def for_leaves(half):
+    def signs(half):
         a = 224 * half
-        act(V("sg", 448 + a, 672 + a), V("sg", a, a + 224), COPY, V("kf", 5, 6))
+        act(V("sg", a, a + 224), PS(4 + half, 224), SIGN)
+        act(V("sg", 448 + a, 672 + a), PS(4 + half, 224), SIGN, V("kf", 5, 6))
+
+    def local_signs(half):
+        a = 224 * half
+        tr(V("tg", 896 + a, 1120 + a), V("sg", a, a + 224))
 
     dma("y", T.lti[:, 0:28], T.lt[:, :], writes=[("lti", range(28))])
     dma("s", T.rti[:, 0:28], T.rt[:, :], writes=[("rti", range(28))])
@@ -218,48 +226,49 @@ def rank_program(g, core, T, topo):
     do("p", lambda e: e.iota(T.pi[:, 0:1], [[0, 1]], 0, 1), V("pi", 0, 1))
     do("p", lambda e: e.iota(T.ci[:, 0:28], [[32, 14], [0, 2]], -896, 0), V("ci", 0, 28))
     do("p", lambda e: e.iota(T.ui[:, 0:8], [[16, 8]], 0, 0), V("ui", 0, 8))
+    do("p", lambda e: e.iota(T.k1[:, 0:4], [[7, 2], [224, 2]], 0, 0, allow_small_or_imprecise_dtypes=True), V("k1", 0, 4))
+    do("p", lambda e: e.iota(T.k2[:, 0:4], [[8, 2], [256, 2]], 5, 0, allow_small_or_imprecise_dtypes=True), V("k2", 0, 4))
     fill(V("one", 0, 512), 1.0)
     for b in range(4):
         do("p", lambda e: e.affine_select(T.et[:, 512 * b:512 * b + 512], T.one[:, 0:512], [[-1, 512]], AluOpType.is_equal, 0.0, b, 4),
            V("et", 512 * b, 512 * b + 512), V("one", 0, 512))
     fill(V("tb0", 0, 448), 0.0)
-    for name, a, b in (("p0", 0, 448), ("gg1", 448, 896), ("h1", 448, 896), ("p1", 0, 448)):
-        act(V(name, a, b), V("tb0", 0, 448), COPY, 0.0)
+    act(V("tb0", 448, 896), V("tb0", 0, 448), COPY, 0.0)
+    for name, a, b in (("xx", 0, 96), ("cw1", 0, 32), ("xy", 0, 64), ("tt", 896, 1344), ("tt", 1344, 1792), ("sg", 896, 912),
+                       ("p0", 0, 448), ("gg1", 448, 896), ("h1", 448, 896), ("p1", 0, 448)):
+        act(V(name, a, b), V("tb0", 448, 448 + b - a), COPY, 0.0)
     for i, (s1, s2, ops) in enumerate([(15, None, (ANDB,)), (4, 1, (SHR, ANDB)), (1, None, (ANDB,)), (31, None, (ANDB,)), (3, None, (ANDB,)), (4, None, (ANDB,))]):
         ts(V("ki", i, i + 1), V("pi", 0, 1), s1, s2, *ops)
-    fill(V("cw", 0, 64), 0.0)
-    fill(V("xx", 0, 96), 0.0)
     cp(V("kf", 0, 6), V("ki", 0, 6))
 
     def K(i):
         return V("kt", i, i + 1)
     X_, H_, B_ = V("kf", 0, 1), V("kf", 1, 2), V("kf", 2, 3)
     tt(K(0), B_, H_, SUB)
-    ts(K(2), H_, -32.0, 98.0, MUL, ADD)
-    ts(K(4), B_, 2.0, -33.0, MUL, ADD)
+    ts(K(2), H_, -32.0, 925.0, MUL, ADD)
+    ts(K(4), B_, 2.0, -860.0, MUL, ADD)
     tt(K(1), K(0), K(0), MUL)
     ts(K(3), B_, -4.0, K(2), MUL, ADD)
+    ts(K(5), K(1), -1.0, None, MUL)
     tt(K(4), K(4), K(3), ADD)
-    tt(K(3), K(3), K(1), MUL)
+    ts(K(3), X_, -14.0, K(3), MUL, ADD)
     tt(K(4), K(4), K(1), MUL)
-    ts(K(3), X_, 2.0, K(3), MUL, ADD)
+    tt(K(3), K(3), K(1), MUL)
     tt(K(4), K(4), X_, ADD)
+    ts(K(3), X_, 16.0, K(3), MUL, ADD)
+    ts(V("k1", 0, 4), V("k1", 0, 4), K(5), K(3), MUL, ADD)
+    tt(V("k1", 0, 4), V("k1", 0, 4), V("k2", 0, 4), ADD)
+    cp(V("cl2", 0, 4), V("k1", 0, 4))
     ts(V("clu", 0, 8), V("ui", 0, 8), V("kf", 4, 5), None, ADD)
-    for k, c in enumerate([0.0, 32.0, 1.0, 33.0]):
-        ts(V("cl2", k, k + 1), K(3), c, None, ADD)
     for k in range(2):
         ts(V("cl1", k, k + 1), K(4), 16.0 * k, None, ADD)
-    ts(V("kf", 6, 7), V("kf", 5, 6), -0.5, 1.0, MUL, ADD)
+    ts(V("kf", 6, 7), V("kf", 5, 6), 0.25, None, MUL)
     ts(V("kf", 5, 6), V("kf", 5, 6), -0.25, 1.0, MUL, ADD)
     ts(V("tb0", 4, 448, 16), V("ci", 0, 28), V("kf", 3, 4), None, ADD)
-    fill(V("sg", 896, 912), 0.0)
-    fill(V("cw1", 0, 32), 0.0)
-    fill(V("xy", 0, 64), 0.0)
-    cp(V("cw", 0, 56, 2), V("lti", 0, 28))
-    cp(V("cw", 1, 56, 2), V("rti", 0, 28))
+    cp(L1, V("lti", 0, 28))
+    cp(R1, V("rti", 0, 28))
     cp(V("nl", 0, 28), V("lti", 0, 28))
-    cp(V("nl", 32, 60), V("rti", 0, 28))
-    conv2(V("nf", 0, 64))
+    conv2("tt", 896, V("nf", 0, 64))
     cp(L0, V("nf", 0, 28))
     cp(R0, V("nf", 32, 60))
     tr(V("ls", 0, 448), V("tb0", 0, 448))
@@ -268,42 +277,45 @@ def rank_program(g, core, T, topo):
     quant("qu", "su", 0, 128, "ut", 0, 512)
     do("v", lambda e: e.tensor_copy(T.qk[:, 0:128].bitcast(dt.uint32), T.qu[:, 0:128].bitcast(dt.uint32).indirect(T.clu[:, 0:8])),
        V("qk", 0, 128), V("qu", 0, 128), V("clu", 0, 8))
-    do("v", lambda e: e.tensor_copy(T.sk[:, 0:128], T.su[:, 0:128].indirect(T.clu[:, 0:8])), V("sk", 0, 128), V("su", 0, 128), V("clu", 0, 8))
+    do("s", lambda e: e.activation(T.sk[:, 0:128], T.su[:, 0:128].indirect(T.clu[:, 0:8]), COPY), V("sk", 0, 128), V("su", 0, 128), V("clu", 0, 8))
     cp(I("p0", 0, 896, "nl", 0, 28), V("ls", 0, 448))
     for h in range(2):
         quant("qx", "sx", 224 * h, 224 * h + 224, "xa", 896 * h, 896 * h + 896)
-    for h in range(2):
         scores(h)
-        for_leaves(h)
+        if h == 0:
+            quant("qe", "se", 0, 512, "et", 0, 2048)
+    for h in range(2):
+        signs(h)
     ahead_lists()
-    tr(V("ta", 0, 448), V("a1", 0, 448))
+    ahead_children()
+    for h in range(2):
+        local_signs(h)
 
     xs, nl = ["xa", "xb"], "nl"
     for k in range(3):
         last = k == 2
         p = T.cores[rank ^ ROUNDS[k]]
         old, new = xs[k % 2], xs[(k + 1) % 2]
-        act(V("gg1", 0, 448), I("sg", 0, 896, nl, 0, 28))
-        cp(V("gg3", 0, 448), I("sg", 0, 912, "pw", 0, 28))
+        w = I("sg", 0, 896, nl, 0, 28)
+        do("s", lambda e: e.activation(T.gg1[:, 0:448], w[0], RELU, bias=T.kf[:, 6:7]), V("gg1", 0, 448), w, V("kf", 6, 7))
+        ts(V("gg3", 0, 448), I("sg", 0, 912, "pw", 0, 28), 0.75, -1.25, MUL, ADD)
         act(V("gg2", 0, 448), I("gg1", 0, 896, nl, 0, 28))
         tr(V("tg", 448, 896), V("gg1", 0, 448))
         tr(V("tg", 1344, 1792), V("gg3", 0, 448))
-        tt(V("dl0", 0, 56), V("ta", 5, 448, 8), LR0, SUB)
-        tt(V("d30", 0, 28), L0, V("ta", 13, 448, 16), SUB)
         tr(V("tg", 0, 448), V("gg2", 0, 448))
-        act(V("tt", 896, 1344), V("tg", 896, 1344))
+        act(V("tt", 896, 1344), V("tg", 896, 1344), RELU)
+        act(V("tt", 902, 1344, 16), V("tg", 898, 1344, 16), RELU, -1.0)
         if k == 0:
             for b in range(4):
                 act(V("win", 896 * b, 896 * b + 448), V("xa", b, 1792, 4), COPY, 0.5)
         else:
             for b in range(4):
                 act(V("win", 896 * b, 896 * b + 224), V(old, b, 896, 4), COPY, 0.5)
-        put = rewrite(V("tg", 896, 1792, 16), V("tg", 452, 1344, 16), [(V("ff", 0, 112, 2), V("ff", 1, 112, 2), V("tg", 1, 896, 16))],
-                      LR0, LR1, "dl0", "d30")
-        put()
+        rewrite(V("tg", 896, 1792, 16), V("tg", 452, 1344, 16), GT, [(V("ff", 0, 112, 2), V("ff", 1, 112, 2), V("tg", 1, 896, 16))],
+                LR0, LR1, "dl0", "d30")
         tr(V("wq", 0, 448), V("tt", 896, 1344))
         act(V("wq", 448, 896), V("wq", 0, 448), COPY, V("kf", 5, 6))
-        conv2(V("nl1", 0, 64))
+        conv2("tt", 896, V("nl1", 0, 64))
         act(V("h1", 0, 448), I("wq", 0, 896, "nl1", 0, 28))
         act(V("h2", 0, 448), I("h1", 0, 896, "nl1", 0, 28))
         cp(I("p1", 0, 896, "nl1", 0, 28), V("wq", 0, 448))
@@ -322,26 +334,25 @@ def rank_program(g, core, T, topo):
         tr(V("tg2", 0, 448), V("h2", 0, 448))
         tr(V("tt", 1344, 1792), V("p1", 0, 448))
         tt(V("dl1", 57, 112, 2), V("tt", 1357, 1792, 16), R1, SUB)
-        put = rewrite(V("tt", 898, 1792, 16), V("tt", 454, 1344, 16),
-                      [(V("ff", 0, 56, 2), V("ff", 1, 56, 2), V("tg2", 3, 448, 16)), (V("ff", 56, 112, 2), V("ff", 57, 112, 2), V("tt", 451, 896, 16))],
-                      LR1, LR0, "dl1", "d31")
+        rewrite(V("tt", 898, 1792, 16), V("tt", 454, 1344, 16), MUL,
+                [(V("ff", 0, 56, 2), V("ff", 1, 56, 2), V("tg2", 3, 448, 16)), (V("ff", 56, 112, 2), V("ff", 57, 112, 2), V("tt", 451, 896, 16))],
+                LR1, LR0, "dl1", "d31")
         nl = "rc%d" % k
-        conv2(V(nl, 0, 64))
+        conv2("tb0", 0, V(nl, 0, 64))
         send(p, T["lr%d" % k][:, 0:28], T[nl][:, 32:60], "aR%d" % k, V(nl, 32, 60))
-        put()
         tr(V("ls", 0, 448), V("tb0", 0, 448))
-        for h in range(2):
+        for h, (c0, c1) in enumerate(PARTS):
             for b in range(4):
-                act(V("zr", 448 * b + 224 * h, 448 * b + 224 * h + 224), I("win", 896 * b, 896 * b + 896, nl, 32 + 14 * h, 46 + 14 * h))
+                act(V("zr", 448 * b + c0, 448 * b + c1), I("win", 896 * b, 896 * b + 896, nl, 32 + c0 // 16, 32 + c1 // 16))
             if h == 0:
                 act(V("ls", 448, 896), V("ls", 0, 448))
-        for h in range(2):
+        for h, (c0, c1) in enumerate(PARTS):
             for b in range(4):
-                o, w = V("zt", 896 * h + b, 896 * h + 896, 4), I("win", 896 * b, 896 * b + 896, nl, 14 * h, 14 * h + 14)
-                tt(o, w, V("zr", 448 * b + 224 * h, 448 * b + 224 * h + 224), ADD)
-            quant("qz", "sz", 224 * h, 224 * h + 224, "zt", 896 * h, 896 * h + 896)
+                o, w = V("zt", 4 * c0 + b, 4 * c1, 4), I("win", 896 * b, 896 * b + 896, nl, c0 // 16, c1 // 16)
+                tt(o, w, V("zr", 448 * b + c0, 448 * b + c1), ADD)
+            quant("qz", "sz", c0, c1, "zt", 4 * c0, 4 * c1)
             for b in range(4):
-                mm(4 * h + b, 224, "qw", "sw", 128 * b, "qz", "sz", 224 * h, 224 * h + 224)
+                mm(4 * h + b, c1 - c0, "qw", "sw", 128 * b, "qz", "sz", c0, c1)
         if last:
             for i, q in enumerate((5, 13)):
                 dma("y", T.gr[:, 448 * i:448 * i + 448], T.ls[q:128:16, 0:448], reads=[("ls", range(448))])
@@ -352,9 +363,9 @@ def rank_program(g, core, T, topo):
         mu, lm = "mu%d" % k, "lm%d" % k
         conv1(V(mu, 0, 32))
         send(p, T[lm][:, 0:14], T[mu][:, 14:28], "aM%d" % k, V(mu, 14, 28))
-        for h in range(2):
+        for h, (c0, c1) in enumerate(PARTS):
             for b in range(4):
-                o, i = V("hw", 448 * b + 224 * h, 448 * b + 224 * h + 224), PS(4 * h + b, 224)
+                o, i = V("hw", 448 * b + c0, 448 * b + c1), PS(4 * h + b, c1 - c0)
                 if h == 0 or b % 2:
                     act(o, i, COPY, 0.03125)
                 else:
@@ -375,9 +386,6 @@ def rank_program(g, core, T, topo):
         for b in range(4):
             tt(V(new, 896 + b, 1792, 4), I("hw", 448 * b, 448 * b + 448, lm, 0, 14), V(old, 896 + b, 1792, 4), ADD)
         quant("qx", "sx", 224, 448, new, 896, 1792)
-        if k == 0:
-            quant("qe", "se", 0, 512, "et", 0, 2048)
-            quant("qv", "sv", 0, 128, "vt", 0, 512)
         if not last:
             scores(1)
             ahead_lists()
@@ -385,9 +393,11 @@ def rank_program(g, core, T, topo):
                 act(V("win", 896 * b + 672, 896 * b + 896), I("hw", 448 * b, 448 * b + 448, lm, 0, 14), COPY, 0.5)
             for b in range(4):
                 act(V("win", 896 * b + 224, 896 * b + 448), V(new, 896 + b, 1792, 4), COPY, 0.5)
-            for_leaves(1)
+            signs(1)
+            local_signs(1)
             act(V("p1", 0, 448), V("ls", 0, 448), COPY, 0.0)
         else:
+            quant("qv", "sv", 0, 128, "vt", 0, 512)
             finish(mm, act, dma, V, PS, T, 1)
         for b in range(4):
             mm(b, 224, "qe", "se", 128 * b, ql, sl, 0, 224)
@@ -395,9 +405,10 @@ def rank_program(g, core, T, topo):
             tt(V(new, b, 896, 4), V(old, b, 896, 4), PS(b, 224), ADD)
         quant("qx", "sx", 0, 224, new, 0, 896)
         if not last:
-            tr(V("ta", 0, 448), V("a1", 0, 448))
             scores(0)
-            for_leaves(0)
+            signs(0)
+            ahead_children()
+            local_signs(0)
         else:
             finish(mm, act, dma, V, PS, T, 0)
     for q in "vstp":

from concourse.mybir import dt, AluOpType, ActivationFunctionType

ROUNDS = [1, 2, 3]
PARTS = [(0, 256), (256, 448)]
ADD, SUB, MUL = AluOpType.add, AluOpType.subtract, AluOpType.mult
GE, GT, LT = AluOpType.is_ge, AluOpType.is_gt, AluOpType.is_lt
NE, ANDB, SHR = AluOpType.not_equal, AluOpType.bitwise_and, AluOpType.arith_shift_right
COPY, RELU, SIGN, MAX = ActivationFunctionType.Copy, ActivationFunctionType.Relu, ActivationFunctionType.Sign, AluOpType.max
F32, BF, I32, U16, U8, MXC = "float32", "bfloat16", "int32", "uint16", "uint8", "float8_e4m3fn_x4"


def _sb(n, d):
    return ("sbuf", [128, n], d)


SCRATCH = {
    "xa": _sb(1792, BF), "xb": _sb(1792, BF), "lvt": _sb(1792, BF), "ut": _sb(512, BF), "vt": _sb(512, BF),
    "one": _sb(512, BF), "et": _sb(2048, BF), "win": _sb(4 * 896, BF), "zr": _sb(1792, BF), "zt": _sb(1792, BF),
    "hw": _sb(1792, BF), "sh": _sb(896, BF), "yb": _sb(448, F32),
    "qu": _sb(128, MXC), "su": _sb(128, U8), "qk": _sb(128, MXC), "sk": _sb(128, U8), "qv": _sb(128, MXC), "sv": _sb(128, U8),
    "qe": _sb(512, MXC), "se": _sb(512, U8), "qw": _sb(512, MXC), "sw": _sb(512, U8), "qx": _sb(448, MXC), "sx": _sb(448, U8),
    "qz": _sb(448, MXC), "sz": _sb(448, U8),
    "lti": _sb(28, I32), "rti": _sb(28, I32), "pi": _sb(1, I32), "ci": _sb(28, I32), "ui": _sb(8, I32), "ki": _sb(7, I32),
    "kf": _sb(7, F32), "kt": _sb(16, F32), "cl2": _sb(4, U16), "cl1": _sb(2, U16), "clu": _sb(8, U16),
    "tb0": _sb(992, F32), "tt": _sb(1888, F32), "k1": _sb(4, F32), "k2": _sb(4, F32), "tg": _sb(1792, BF), "tg2": _sb(448, BF), "ta": _sb(448, F32), "tp": _sb(448, F32),
    "tm": _sb(448, F32), "ls": _sb(896, F32), "wq": _sb(896, F32), "sg": _sb(912, BF), "gg1": _sb(896, BF), "gg2": _sb(448, BF),
    "gg3": _sb(448, BF), "h1": _sb(896, F32), "h2": _sb(448, BF), "p0": _sb(896, F32), "p1": _sb(896, F32), "a1": _sb(448, F32),
    "ms": _sb(448, F32), "xx": _sb(96, F32), "cw1": _sb(96, F32), "xy": _sb(64, F32),
    "nl": _sb(64, U16), "nl1": _sb(64, U16), "nf": _sb(64, F32), "pw": _sb(32, U16),
    "t28": _sb(28, F32), "ff": _sb(112, F32), "pr": _sb(112, F32), "p3": _sb(28, F32), "uu": _sb(56, F32),
    "dl0": _sb(112, F32), "dl1": _sb(112, F32), "d30": _sb(28, F32), "d31": _sb(28, F32),
    "ps": ("psum", [128, 4096], F32),
}
for _k in range(3):
    SCRATCH.update({"rc%d" % _k: _sb(64, U16), "mu%d" % _k: _sb(32, U16), "lr%d" % _k: _sb(28, U16), "lm%d" % _k: _sb(14, U16),
                    "qs%d" % _k: _sb(224, MXC), "ss%d" % _k: _sb(224, U8), "ql%d" % _k: _sb(224, MXC), "sl%d" % _k: _sb(224, U8)})
ENG_SEM = {"v": "eV", "s": "eS", "t": "eT", "p": "eP"}
SEMAPHORES = list(ENG_SEM.values()) + ["loc"] + ["d%d" % i for i in range(32)] + ["%s%d" % (a, k) for a in ("aR", "aM", "aC", "aS") for k in range(3)]


def rank_program(g, core, T, topo):
    rank = T.rank_of(core)
    if rank is None:
        return
    eng = {"v": g.vector, "s": g.scalar, "t": g.tensor, "p": g, "y": g.sync}
    cnt = {"v": 0, "s": 0, "t": 0, "p": 0}
    know = {q: {} for q in eng}
    snap, recs, ndma, nloc = {}, {}, [0], [0]

    def wait(q, sem, val):
        if know[q].get(sem, 0) >= val:
            return
        eng[q].wait_ge(T.sem[sem], val)
        for s, n in snap.get((sem, val), {}).items():
            know[q][s] = max(know[q].get(s, 0), n)
        know[q][sem] = max(know[q].get(sem, 0), val)

    def need(q, src, reads, writes):
        w = {}
        for acc, wr in [(a, False) for a in reads] + [(a, True) for a in writes]:
            name, cols = acc
            for rn, rcols, rwr, rsrc, sem, val in recs.get(name, []):
                if name == "ps":
                    if rsrc == src or not (cols & rcols):
                        continue
                elif not (wr or rwr) or not (cols & rcols):
                    continue
                elif rsrc == src and not rwr:
                    continue
                w[sem] = max(w.get(sem, 0), val)
        for sem in sorted(w):
            wait(q, sem, w[sem])

    def note(src, sem, val, reads, writes):
        for name, cols in writes:
            recs[name] = [r for r in recs.get(name, []) if not (r[1] <= cols)]
        for name, cols in reads:
            recs[name] = [r for r in recs.get(name, []) if not (not r[2] and r[3] == src and src != "dma" and r[1] <= cols)]
        for acc, wr in [(a, False) for a in reads] + [(a, True) for a in writes]:
            recs.setdefault(acc[0], []).append((acc[0], acc[1], wr, src, sem, val))

    def acc(*views):
        out = []
        for v in views:
            for name, cols in v[1]:
                if name == "ps":
                    cols = frozenset(x // 512 for x in cols)
                out.append((name, frozenset(cols)))
        return out

    def V(name, a, b, s=1):
        return (T[name][:, a:b] if s == 1 else T[name][:, a:b:s], [(name, range(a, b, s))])

    def I(name, a, b, off, c, d):
        return (T[name][:, a:b].indirect(T[off][:, c:d]), [(name, range(a, b)), (off, range(c, d))])

    def do(q, call, out, *ins):
        outs = list(out) if isinstance(out, list) else [out]
        reads, writes = [], acc(*[(o[0], o[1][:1]) for o in outs])
        for o in outs:
            reads += acc((None, o[1][1:]))
        reads += acc(*ins)
        need(q, q, reads, writes)
        r = call(eng[q])
        cnt[q] += 1
        sem = ENG_SEM[q]
        r.then_inc(T.sem[sem], 1)
        k = dict(know[q])
        k[sem] = cnt[q]
        snap[(sem, cnt[q])] = k
        note(q, sem, cnt[q], reads, writes)

    def dma(q, out_ap, in_ap, reads=(), writes=()):
        need(q, "dma", acc((None, reads)), acc((None, writes)))
        sem = "d%d" % ndma[0]
        ndma[0] += 1
        eng[q].dma_start(out_ap, in_ap).then_inc(T.sem[sem], 16)
        snap[(sem, 16)] = dict(know[q])
        note("dma", sem, 16, acc((None, reads)), acc((None, writes)))

    def send(dst, out_ap, in_ap, sem, view):
        need("p", "rem", acc(view), [])
        a = topo.addr(dst)
        g.remote_dma(out_ap, in_ap, T.sem[sem], T.sem["loc"], a[1], a[0], topo.mask(core, dst))
        nloc[0] += len(topo.engines(core, dst))

    def lands(name, n, sem, src):
        recs.setdefault(name, []).append((name, frozenset(range(n)), True, "rem", sem, len(topo.engines(src, core))))

    def tt(out, a, b, op):
        do("v", lambda e: e.tensor_tensor(out[0], a[0], b[0], op), out, a, b)

    def ts(out, a, s1, s2, op0, *op1):
        sc = [x for x in (s1, s2) if isinstance(x, tuple)]
        do("v", lambda e: e.tensor_scalar(out[0], a[0], s1[0] if isinstance(s1, tuple) else s1, s2[0] if isinstance(s2, tuple) else s2, op0, *op1), out, a, *sc)

    def cp(out, a):
        do("v", lambda e: e.tensor_copy(out[0], a[0]), out, a)

    def tr(out, a):
        do("v", lambda e: e.transpose(out[0], a[0]), out, a)

    def fill(out, c):
        do("v", lambda e: e.memset(out[0], c), out)

    def act(out, a, func=COPY, scale=1.0):
        if isinstance(scale, tuple):
            do("s", lambda e: e.activation(out[0], a[0], func, scale=scale[0]), out, a, scale)
        else:
            do("s", lambda e: e.activation(out[0], a[0], func, scale=scale), out, a)

    def quant(q, s, a, b, tile, ta, tb):
        do("v", lambda e: e.quantize_mx(T[q][:, a:b], T[s][:, a:b], T[tile][:, ta:tb]), [V(q, a, b), V(s, a, b)], V(tile, ta, tb))

    def mm(bank, n, ql, sl, la, qr, sr, a, b):
        o = V("ps", 512 * bank, 512 * bank + n)
        do("t", lambda e: e.matmul_mx(o[0], T[ql][:, la:la + 128], T[sl][:, la:la + 128], T[qr][:, a:b], T[sr][:, a:b], True, True), o,
           V(ql, la, la + 128), V(sl, la, la + 128), V(qr, a, b), V(sr, a, b))

    def PS(bank, n):
        return V("ps", 512 * bank, 512 * bank + n)

    def conv2(buf, o, out):
        tr(V("xx", 16, 80), V(buf, o + 5, o + 510, 8))
        tr(V(buf, o + 896, o + 992), V("xx", 0, 96))
        cp(out, I(buf, o, o + 992, "cl2", 0, 4))

    def conv1(out):
        tr(V("xy", 16, 48), V("cw1", 0, 32))
        tr(V("cw1", 32, 96), V("xy", 0, 64))
        cp(out, I("cw1", 0, 96, "cl1", 0, 2))

    def rewrite(plus, minus, acting, turns, base, nxt, dl, d3):
        tt(V("ff", 1, 112, 2), plus, minus, acting)
        for o, i, a in turns:
            tt(o, i, a, MUL)
        tt(V("pr", 0, 112), V("ff", 0, 112), V(dl, 0, 112), MUL)
        tt(V("p3", 0, 28), V("ff", 0, 56, 2), V(d3, 0, 28), MUL)
        tt(V("uu", 0, 56), V("pr", 0, 56), V("pr", 56, 112), ADD)
        tt(V("uu", 1, 56, 2), V("uu", 1, 56, 2), V("p3", 0, 28), ADD)
        tt(nxt, base, V("uu", 0, 56), ADD)

    L0, R0, LR0 = V("tb0", 5, 448, 16), V("tb0", 13, 448, 16), V("tb0", 5, 448, 8)
    L1, R1, LR1 = V("tt", 901, 1344, 16), V("tt", 909, 1344, 16), V("tt", 901, 1344, 8)

    def ahead_lists():
        tr(V("tp", 0, 448), V("p0", 0, 448))
        ts(V("cw1", 0, 28), V("tp", 4, 448, 16), 896.0, None, ADD)
        conv1(V("pw", 0, 32))
        tt(V("dl0", 56, 112, 2), R0, L0, SUB)
        tt(V("dl0", 57, 112, 2), V("tp", 13, 448, 16), R0, SUB)

    def ahead_children():
        tr(V("ta", 0, 448), V("a1", 0, 448))
        tt(V("dl0", 0, 56), V("ta", 5, 448, 8), LR0, SUB)
        tt(V("d30", 0, 28), L0, V("ta", 13, 448, 16), SUB)

    def scores(half):
        a = 224 * half
        mm(4 + half, 224, "qk", "sk", 0, "qx", "sx", a, a + 224)

    def signs(half):
        a = 224 * half
        act(V("sg", a, a + 224), PS(4 + half, 224), SIGN)
        act(V("sg", 448 + a, 672 + a), PS(4 + half, 224), SIGN, V("kf", 5, 6))

    def local_signs(half):
        a = 224 * half
        tr(V("tg", 896 + a, 1120 + a), V("sg", a, a + 224))

    dma("y", T.lti[:, 0:28], T.lt[:, :], writes=[("lti", range(28))])
    dma("s", T.rti[:, 0:28], T.rt[:, :], writes=[("rti", range(28))])
    dma("s", T.ut[:, :], T.u[:, :], writes=[("ut", range(512))])
    for h in range(2):
        dma("y", T.xa[:, 896 * h:896 * h + 896], T.x[:, 896 * h:896 * h + 896], writes=[("xa", range(896 * h, 896 * h + 896))])
    dma("s", T.lvt[:, :], T.lv[:, :], writes=[("lvt", range(1792))])
    dma("y", T.qw[:, 0:512].bitcast(dt.uint8), T.wc[:, :], writes=[("qw", range(512))])
    dma("y", T.sw[:, 0:512], T.ws[:, :], writes=[("sw", range(512))])
    dma("y", T.vt[:, :], T.v[:, :], writes=[("vt", range(512))])
    for k in range(3):
        p = T.cores[rank ^ ROUNDS[k]]
        lands("lr%d" % k, 28, "aR%d" % k, p)
        lands("lm%d" % k, 14, "aM%d" % k, p)
        lands("ql%d" % k, 224, "aC%d" % k, p)
        lands("sl%d" % k, 224, "aS%d" % k, p)
    do("p", lambda e: e.iota(T.pi[:, 0:1], [[0, 1]], 0, 1), V("pi", 0, 1))
    do("p", lambda e: e.iota(T.ci[:, 0:28], [[32, 14], [0, 2]], -896, 0), V("ci", 0, 28))
    do("p", lambda e: e.iota(T.ui[:, 0:8], [[16, 8]], 0, 0), V("ui", 0, 8))
    do("p", lambda e: e.iota(T.k1[:, 0:4], [[7, 2], [224, 2]], 0, 0, allow_small_or_imprecise_dtypes=True), V("k1", 0, 4))
    do("p", lambda e: e.iota(T.k2[:, 0:4], [[8, 2], [256, 2]], 5, 0, allow_small_or_imprecise_dtypes=True), V("k2", 0, 4))
    fill(V("one", 0, 512), 1.0)
    for b in range(4):
        do("p", lambda e: e.affine_select(T.et[:, 512 * b:512 * b + 512], T.one[:, 0:512], [[-1, 512]], AluOpType.is_equal, 0.0, b, 4),
           V("et", 512 * b, 512 * b + 512), V("one", 0, 512))
    fill(V("tb0", 0, 448), 0.0)
    act(V("tb0", 448, 896), V("tb0", 0, 448), COPY, 0.0)
    for name, a, b in (("xx", 0, 96), ("cw1", 0, 32), ("xy", 0, 64), ("tt", 896, 1344), ("tt", 1344, 1792), ("sg", 896, 912),
                       ("p0", 0, 448), ("gg1", 448, 896), ("h1", 448, 896), ("p1", 0, 448)):
        act(V(name, a, b), V("tb0", 448, 448 + b - a), COPY, 0.0)
    for i, (s1, s2, ops) in enumerate([(15, None, (ANDB,)), (4, 1, (SHR, ANDB)), (1, None, (ANDB,)), (31, None, (ANDB,)), (3, None, (ANDB,)), (4, None, (ANDB,))]):
        ts(V("ki", i, i + 1), V("pi", 0, 1), s1, s2, *ops)
    cp(V("kf", 0, 6), V("ki", 0, 6))

    def K(i):
        return V("kt", i, i + 1)
    X_, H_, B_ = V("kf", 0, 1), V("kf", 1, 2), V("kf", 2, 3)
    tt(K(0), B_, H_, SUB)
    ts(K(2), H_, -32.0, 925.0, MUL, ADD)
    ts(K(4), B_, 2.0, -860.0, MUL, ADD)
    tt(K(1), K(0), K(0), MUL)
    ts(K(3), B_, -4.0, K(2), MUL, ADD)
    ts(K(5), K(1), -1.0, None, MUL)
    tt(K(4), K(4), K(3), ADD)
    ts(K(3), X_, -14.0, K(3), MUL, ADD)
    tt(K(4), K(4), K(1), MUL)
    tt(K(3), K(3), K(1), MUL)
    tt(K(4), K(4), X_, ADD)
    ts(K(3), X_, 16.0, K(3), MUL, ADD)
    ts(V("k1", 0, 4), V("k1", 0, 4), K(5), K(3), MUL, ADD)
    tt(V("k1", 0, 4), V("k1", 0, 4), V("k2", 0, 4), ADD)
    cp(V("cl2", 0, 4), V("k1", 0, 4))
    ts(V("clu", 0, 8), V("ui", 0, 8), V("kf", 4, 5), None, ADD)
    for k in range(2):
        ts(V("cl1", k, k + 1), K(4), 16.0 * k, None, ADD)
    ts(V("kf", 6, 7), V("kf", 5, 6), 0.25, None, MUL)
    ts(V("kf", 5, 6), V("kf", 5, 6), -0.25, 1.0, MUL, ADD)
    ts(V("tb0", 4, 448, 16), V("ci", 0, 28), V("kf", 3, 4), None, ADD)
    cp(L1, V("lti", 0, 28))
    cp(R1, V("rti", 0, 28))
    cp(V("nl", 0, 28), V("lti", 0, 28))
    conv2("tt", 896, V("nf", 0, 64))
    cp(L0, V("nf", 0, 28))
    cp(R0, V("nf", 32, 60))
    tr(V("ls", 0, 448), V("tb0", 0, 448))
    act(V("ls", 448, 896), V("ls", 0, 448))
    act(V("a1", 0, 448), I("ls", 0, 896, "nl", 0, 28))
    quant("qu", "su", 0, 128, "ut", 0, 512)
    do("v", lambda e: e.tensor_copy(T.qk[:, 0:128].bitcast(dt.uint32), T.qu[:, 0:128].bitcast(dt.uint32).indirect(T.clu[:, 0:8])),
       V("qk", 0, 128), V("qu", 0, 128), V("clu", 0, 8))
    do("s", lambda e: e.activation(T.sk[:, 0:128], T.su[:, 0:128].indirect(T.clu[:, 0:8]), COPY), V("sk", 0, 128), V("su", 0, 128), V("clu", 0, 8))
    cp(I("p0", 0, 896, "nl", 0, 28), V("ls", 0, 448))
    for h in range(2):
        quant("qx", "sx", 224 * h, 224 * h + 224, "xa", 896 * h, 896 * h + 896)
        scores(h)
        if h == 0:
            quant("qe", "se", 0, 512, "et", 0, 2048)
    for h in range(2):
        signs(h)
    ahead_lists()
    ahead_children()
    for h in range(2):
        local_signs(h)

    xs, nl = ["xa", "xb"], "nl"
    for k in range(3):
        last = k == 2
        p = T.cores[rank ^ ROUNDS[k]]
        old, new = xs[k % 2], xs[(k + 1) % 2]
        w = I("sg", 0, 896, nl, 0, 28)
        do("s", lambda e: e.activation(T.gg1[:, 0:448], w[0], RELU, bias=T.kf[:, 6:7]), V("gg1", 0, 448), w, V("kf", 6, 7))
        ts(V("gg3", 0, 448), I("sg", 0, 912, "pw", 0, 28), 0.75, -1.25, MUL, ADD)
        act(V("gg2", 0, 448), I("gg1", 0, 896, nl, 0, 28))
        tr(V("tg", 448, 896), V("gg1", 0, 448))
        tr(V("tg", 1344, 1792), V("gg3", 0, 448))
        tr(V("tg", 0, 448), V("gg2", 0, 448))
        act(V("tt", 896, 1344), V("tg", 896, 1344), RELU)
        act(V("tt", 902, 1344, 16), V("tg", 898, 1344, 16), RELU, -1.0)
        if k == 0:
            for b in range(4):
                act(V("win", 896 * b, 896 * b + 448), V("xa", b, 1792, 4), COPY, 0.5)
        else:
            for b in range(4):
                act(V("win", 896 * b, 896 * b + 224), V(old, b, 896, 4), COPY, 0.5)
        rewrite(V("tg", 896, 1792, 16), V("tg", 452, 1344, 16), GT, [(V("ff", 0, 112, 2), V("ff", 1, 112, 2), V("tg", 1, 896, 16))],
                LR0, LR1, "dl0", "d30")
        tr(V("wq", 0, 448), V("tt", 896, 1344))
        act(V("wq", 448, 896), V("wq", 0, 448), COPY, V("kf", 5, 6))
        conv2("tt", 896, V("nl1", 0, 64))
        act(V("h1", 0, 448), I("wq", 0, 896, "nl1", 0, 28))
        act(V("h2", 0, 448), I("h1", 0, 896, "nl1", 0, 28))
        cp(I("p1", 0, 896, "nl1", 0, 28), V("wq", 0, 448))
        if k == 0:
            for b in range(4):
                act(V("win", 896 * b + 448, 896 * b + 896), V("lvt", b, 1792, 4), COPY, 0.5)
        else:
            for b in range(4):
                act(V("win", 896 * b + 448, 896 * b + 672), PS(b, 224), COPY, 0.5)
        if not last:
            act(V("p0", 0, 448), V("wq", 0, 448), COPY, 0.0)
        tt(V("dl1", 56, 112, 2), R1, L1, SUB)
        tr(V("tt", 448, 896), V("h1", 0, 448))
        tt(V("dl1", 0, 56), V("tt", 453, 896, 8), LR1, SUB)
        tt(V("d31", 0, 28), L1, V("tt", 461, 896, 16), SUB)
        tr(V("tg2", 0, 448), V("h2", 0, 448))
        tr(V("tt", 1344, 1792), V("p1", 0, 448))
        tt(V("dl1", 57, 112, 2), V("tt", 1357, 1792, 16), R1, SUB)
        rewrite(V("tt", 898, 1792, 16), V("tt", 454, 1344, 16), MUL,
                [(V("ff", 0, 56, 2), V("ff", 1, 56, 2), V("tg2", 3, 448, 16)), (V("ff", 56, 112, 2), V("ff", 57, 112, 2), V("tt", 451, 896, 16))],
                LR1, LR0, "dl1", "d31")
        nl = "rc%d" % k
        conv2("tb0", 0, V(nl, 0, 64))
        send(p, T["lr%d" % k][:, 0:28], T[nl][:, 32:60], "aR%d" % k, V(nl, 32, 60))
        tr(V("ls", 0, 448), V("tb0", 0, 448))
        for h, (c0, c1) in enumerate(PARTS):
            for b in range(4):
                act(V("zr", 448 * b + c0, 448 * b + c1), I("win", 896 * b, 896 * b + 896, nl, 32 + c0 // 16, 32 + c1 // 16))
            if h == 0:
                act(V("ls", 448, 896), V("ls", 0, 448))
        for h, (c0, c1) in enumerate(PARTS):
            for b in range(4):
                o, w = V("zt", 4 * c0 + b, 4 * c1, 4), I("win", 896 * b, 896 * b + 896, nl, c0 // 16, c1 // 16)
                tt(o, w, V("zr", 448 * b + c0, 448 * b + c1), ADD)
            quant("qz", "sz", c0, c1, "zt", 4 * c0, 4 * c1)
            for b in range(4):
                mm(4 * h + b, c1 - c0, "qw", "sw", 128 * b, "qz", "sz", c0, c1)
        if last:
            for i, q in enumerate((5, 13)):
                dma("y", T.gr[:, 448 * i:448 * i + 448], T.ls[q:128:16, 0:448], reads=[("ls", range(448))])
        act(V("ms", 0, 448), I("ls", 0, 896, "lr%d" % k, 0, 28))
        tr(V("tm", 0, 448), V("ms", 0, 448))
        ts(V("t28", 0, 28), V("tm", 5, 448, 16), 448.0, -448.0, GE, MUL)
        tt(V("cw1", 0, 28), V("tm", 5, 448, 16), V("t28", 0, 28), ADD)
        mu, lm = "mu%d" % k, "lm%d" % k
        conv1(V(mu, 0, 32))
        send(p, T[lm][:, 0:14], T[mu][:, 14:28], "aM%d" % k, V(mu, 14, 28))
        for h, (c0, c1) in enumerate(PARTS):
            for b in range(4):
                o, i = V("hw", 448 * b + c0, 448 * b + c1), PS(4 * h + b, c1 - c0)
                if h == 0 or b % 2:
                    act(o, i, COPY, 0.03125)
                else:
                    ts(o, i, 0.03125, None, MUL)
        for b in range(4):
            o, w = V("sh", b, 896, 4), I("hw", 448 * b, 448 * b + 448, mu, 0, 14)
            if b % 2:
                act(o, w)
            else:
                cp(o, w)
        qs, ss, ql, sl = "qs%d" % k, "ss%d" % k, "ql%d" % k, "sl%d" % k
        quant(qs, ss, 0, 224, "sh", 0, 896)
        send(p, T[ql][:, 0:224].bitcast(dt.uint8), T[qs][:, 0:224].bitcast(dt.uint8), "aC%d" % k, V(qs, 0, 224))
        send(p, T[sl][:, 0:224], T[ss][:, 0:224], "aS%d" % k, V(ss, 0, 224))
        if not last:
            cp(I("p0", 0, 896, nl, 0, 28), V("ls", 0, 448))
            act(V("a1", 0, 448), I("ls", 0, 896, nl, 0, 28))
        for b in range(4):
            tt(V(new, 896 + b, 1792, 4), I("hw", 448 * b, 448 * b + 448, lm, 0, 14), V(old, 896 + b, 1792, 4), ADD)
        quant("qx", "sx", 224, 448, new, 896, 1792)
        if not last:
            scores(1)
            ahead_lists()
            for b in range(4):
                act(V("win", 896 * b + 672, 896 * b + 896), I("hw", 448 * b, 448 * b + 448, lm, 0, 14), COPY, 0.5)
            for b in range(4):
                act(V("win", 896 * b + 224, 896 * b + 448), V(new, 896 + b, 1792, 4), COPY, 0.5)
            signs(1)
            local_signs(1)
            act(V("p1", 0, 448), V("ls", 0, 448), COPY, 0.0)
        else:
            quant("qv", "sv", 0, 128, "vt", 0, 512)
            finish(mm, act, dma, V, PS, T, 1)
        for b in range(4):
            mm(b, 224, "qe", "se", 128 * b, ql, sl, 0, 224)
        for b in range(4):
            tt(V(new, b, 896, 4), V(old, b, 896, 4), PS(b, 224), ADD)
        quant("qx", "sx", 0, 224, new, 0, 896)
        if not last:
            scores(0)
            signs(0)
            ahead_children()
            local_signs(0)
        else:
            finish(mm, act, dma, V, PS, T, 0)
    for q in "vstp":
        wait("y", ENG_SEM[q], cnt[q])
    for i in range(ndma[0]):
        wait("y", "d%d" % i, 16)
    g.wait_ge(T.sem["loc"], nloc[0])


def finish(mm, act, dma, V, PS, T, half):
    a, b = 224 * half, 224 * half + 224
    mm(4 + half, 224, "qv", "sv", 0, "qx", "sx", a, b)
    dma("y", T.oc[:, 4 * a:4 * b], T.qx[:, a:b].bitcast(dt.uint8), reads=[("qx", range(a, b))])
    for k in range(4):
        dma("y", T.osc[4 * k:4 * k + 4, a:b], T.sx[32 * k:32 * k + 4, a:b], reads=[("sx", range(a, b))])
    act(V("yb", a, b), PS(4 + half, 224))
    dma("s", T.y[:, a:b], T.yb[:, a:b], reads=[("yb", range(a, b))])
